import numpy as np
import ml_dtypes


def mxq(x, axis, fmt="e4m3"):
    dtype, down = {"e4m3": (ml_dtypes.float8_e4m3fn, 7), "e5m2": (ml_dtypes.float8_e5m2, 14)}[fmt]
    v = np.moveaxis(np.asarray(x, np.float32).astype(ml_dtypes.bfloat16).astype(np.float64), axis, -1)
    blocks = v.reshape(v.shape[:-1] + (-1, 32))
    amax = np.abs(blocks).max(-1, keepdims=True)
    byte = np.maximum(np.where(amax > 0, np.frexp(amax)[1] - 1 + 127, 0) - down, 1)
    scale = np.exp2(byte - 127.0)
    codes = (blocks / scale).astype(np.float32).astype(dtype).astype(np.float64)
    return np.moveaxis((codes * scale).reshape(v.shape), -1, axis)


WIDE = False


def mx_kscale(k):
    if not WIDE:
        return np.ones(k)
    levels = np.array([10, -10, 5, -5, 0])
    if k % 512:
        return np.exp2(np.random.permutation(np.resize(levels, k // 32))).repeat(32)
    a = np.empty((k // 512, 16))
    for p in range(k // 512):
        a[p, :8] = np.random.permutation(np.resize(levels, 8))
        for g in range(8):
            far = levels[np.abs(levels - a[p, g]) >= 10]
            a[p, g + 8] = far[np.random.randint(len(far))]
    return np.exp2(a.ravel()).repeat(32)


def f64(x):
    return np.asarray(x).astype(np.float64)


def striped(idx):
    return np.tile(idx.reshape(-1, 16).T, (8, 1)).astype(np.uint16)


def unstriped(offs):
    return offs[:16].T.reshape(-1).astype(np.int64)


def pack_weight(w):
    k, n = w.shape
    w = f64(np.asarray(w, np.float32).astype(ml_dtypes.bfloat16)).reshape(k // 32, 32, n)
    amax = np.abs(w).max(1)
    byte = np.clip(np.where(amax > 0, np.frexp(amax)[1] - 1 + 127 - 7, 1), 1, 254)
    scaled = (w * np.exp2(127.0 - byte)[:, None, :]).reshape(k, n).astype(np.float32)
    words = np.ascontiguousarray(scaled.reshape(k // 512, 128, 4, n).transpose(0, 1, 3, 2)).astype(ml_dtypes.float8_e4m3fn).view(np.uint8)
    return words, np.ascontiguousarray(byte.astype(np.uint8).reshape(k // 512, 16, n))


def unpack_weight(words, scales):
    g, p, n, _ = words.shape
    vals = np.ascontiguousarray(words).view(ml_dtypes.float8_e4m3fn).astype(np.float64) * np.repeat(np.exp2(scales.astype(np.float64) - 127.0), 8, axis=1)[..., None]
    return vals.transpose(0, 1, 3, 2).reshape(g * 512, n)


def sigmoid(v):
    return 1.0 / (1.0 + np.exp(-np.maximum(v, -700.0)))


K, T, S, V, U, D = 512, 1024, 512, 512, 512, 4


def setup_inputs():
    n = np.random.standard_normal
    s = mx_kscale(K)[:, None]
    packed_xT = pack_weight(n((K, T)) * s)
    return {
        "x_words": packed_xT[0],
        "x_scales": packed_xT[1],
        "hT": (n((K, V)) / np.sqrt(K) / s).astype(np.float32),
        "offs": striped(np.random.permutation(T)[:S]),
        "code": striped(np.random.randint(0, S, U)),
    }


def reference(x_words, x_scales, hT, offs, code):
    hTq = mxq(f64(hT), 0, "e4m3")
    xq = unpack_weight(x_words, x_scales)[:, unstriped(offs)]
    y = hTq.T @ xq
    top = y.max(axis=1, keepdims=True)
    p = y * (sigmoid(6.0 * (y - (0.4 * top))))
    gg = p[:, unstriped(code)]
    return gg.reshape(len(gg), -1, D).max(axis=2) + 0.25 * (gg.reshape(len(gg), -1, D).mean(axis=2))

@@ -1,0 +1,161 @@
+from contextlib import ExitStack
+
+import concourse.mybir as mybir
+from concourse.masks import make_identity
+
+K, T, S, V, U, D = 512, 1024, 512, 512, 512, 4
+FLOPS = 2 * K * V * S
+
+F32 = mybir.dt.float32
+BF16 = mybir.dt.bfloat16
+I32 = mybir.dt.int32
+U32 = mybir.dt.uint32
+U16 = mybir.dt.uint16
+U8 = mybir.dt.uint8
+FP8X4 = mybir.dt.float8_e4m3fn_x4
+ALU = mybir.AluOpType
+ACT = mybir.ActivationFunctionType
+
+P = 128
+PACK = 4
+TILES = V // P
+PASSAGES = U // D
+HALF = U // 2
+LIST_ROWS = 16
+
+
+def tile_picked_yplaid_mix_p_kernel(tc, x_words, x_scales, hT, offs, code, out):
+    nc = tc.nc
+    with ExitStack() as ctx:
+        lists = ctx.enter_context(tc.tile_pool(name="lists", bufs=1))
+        sb = ctx.enter_context(tc.tile_pool(name="sb", bufs=1))
+        psum = ctx.enter_context(tc.psum_pool(name="psum", bufs=1))
+
+        offs_sb = lists.tile([P, S // LIST_ROWS], U16, name="offs_sb")
+        code_sb = lists.tile([P, U // LIST_ROWS], U16, name="code_sb")
+        all_words = sb.tile([P, T], U32, name="all_words")
+        all_scales = sb.tile([P, T], U8, name="all_scales")
+        x_codes = sb.tile([P, S], U32, name="x_codes", align_bytes=64)
+        x_plane = sb.tile([P, S], U8, name="x_plane", align_bytes=64)
+        ident = sb.tile([P, P], F32, name="ident")
+
+        def tiles(pool, stem, shape, dtype, count=TILES, **kw):
+            return [pool.tile(shape, dtype, name=f"{stem}{i}", **kw) for i in range(count)]
+
+        h_raw = tiles(sb, "h_raw", [P, PACK, P], F32)
+        h_bf = tiles(sb, "h_bf", [P, P, PACK], BF16, align_bytes=64)
+        h_codes = tiles(sb, "h_codes", [P, P], U32, align_bytes=64)
+        h_plane = tiles(sb, "h_plane", [P, P], U8, align_bytes=64)
+        y = tiles(psum, "y", [P, S], F32)
+        u = tiles(sb, "u", [P, S], F32)
+        bias = tiles(sb, "bias", [P, 1], F32)
+        tops = tiles(sb, "tops", [P, 1], F32)
+        gate = tiles(sb, "gate", [P, S], F32)
+        p = tiles(sb, "p", [P, S], F32)
+        gg = tiles(sb, "gg", [P, PASSAGES, D], F32)
+        pair_max = {TILES - 1: sb.tile([P, PASSAGES, 2], F32, name="pair_max")}
+        best = tiles(sb, "best", [P, PASSAGES], F32)
+        res = tiles(sb, "res", [P, PASSAGES], F32)
+        mean_t = tiles(sb, "mean_t", [P, P], F32, count=TILES - 1)
+        pair_sum = sb.tile([P, PASSAGES, 2], F32, name="pair_sum")
+        last_sum = sb.tile([P, PASSAGES], F32, name="last_sum")
+
+        nc.gpsimd.memset(all_scales[:].bitcast(I32), 0)
+        nc.sync.dma_start(offs_sb[:], offs)
+        nc.sync.dma_start(all_words[:].bitcast(I32), x_words[0].rearrange("p n t -> p (n t)").bitcast(I32))
+        for q in range(4):
+            nc.sync.dma_start(
+                all_scales[32 * q : 32 * q + 4, :].bitcast(I32),
+                x_scales[0, 4 * q : 4 * q + 4, :].bitcast(I32),
+            )
+        h_view = hT.rearrange("(p j) w -> p j w", j=PACK)
+        for i in range(TILES):
+            nc.sync.dma_start(h_raw[i][:], h_view[:, :, i * P : (i + 1) * P])
+        nc.sync.dma_start(code_sb[:], code)
+        make_identity(nc, ident[:])
+
+        def interleave(i):
+            nc.scalar.copy(h_bf[i][:], h_raw[i][:].rearrange("p j w -> p w j"))
+
+        def quantise(i):
+            nc.vector.quantize_mx(
+                out=h_codes[i][:].bitcast(FP8X4),
+                scales=h_plane[i][:],
+                in_=h_bf[i][:].rearrange("p w j -> p (w j)"),
+            )
+
+        def score(i):
+            nc.tensor.matmul_mx(
+                out=y[i][:],
+                lhsT=h_codes[i][:].bitcast(FP8X4),
+                lhsT_scale=h_plane[i][:],
+                rhs=x_codes[:].bitcast(FP8X4),
+                rhs_scale=x_plane[:],
+                start=True,
+                stop=True,
+            )
+
+        def top(i):
+            nc.vector.tensor_scalar(u[i][:], y[i][:], 1.0, None, ALU.mult, ALU.max, accum_out=tops[i][:])
+            nc.scalar.activation(bias[i][:], tops[i][:], ACT.Copy, scale=-2.4)
+            nc.scalar.activation(gate[i][:], u[i][:], ACT.Sigmoid, bias=bias[i][:], scale=6.0)
+            nc.gpsimd.tensor_tensor(p[i][:], u[i][:], gate[i][:], ALU.mult)
+
+        def fetch(i):
+            flat = gg[i][:].rearrange("p v d -> p (v d)")
+            cols = HALF // LIST_ROWS
+            for h in range(2):
+                nc.vector.tensor_copy(
+                    flat[:, h * HALF : (h + 1) * HALF],
+                    p[i][:].indirect(code_sb[:, h * cols : (h + 1) * cols]),
+                )
+
+        mean = {}
+
+        def sum_on_tensor(i):
+            sum_t = psum.tile([P, P], F32, name="sum_t", bufs=2)
+            for d in range(D):
+                nc.tensor.matmul(sum_t[:], gg[i][:, :, d], ident[:], start=(d == 0), stop=(d == D - 1), is_transpose=True)
+            nc.scalar.activation(mean_t[i][:], sum_t[:], ACT.Copy, scale=0.25 / D)
+            back = psum.tile([P, P], F32, name="back", bufs=2)
+            nc.tensor.transpose(back[:], mean_t[i][:], ident[:])
+            mean[i] = back
+
+        def max_pairs(i):
+            nc.vector.tensor_tensor(pair_max[i][:], gg[i][:, :, 0:2], gg[i][:, :, 2:4], ALU.max)
+
+        def max_final(i):
+            nc.vector.tensor_tensor(best[i][:], pair_max[i][:, :, 0], pair_max[i][:, :, 1], ALU.max)
+
+        def store(i):
+            nc.sync.dma_start(out[i * P : (i + 1) * P, :], res[i][:])
+
+        def finish(i):
+            nc.vector.tensor_tensor(res[i][:], mean[i][:], best[i][:], ALU.add)
+            store(i)
+
+        for i in range(TILES):
+            interleave(i)
+        nc.vector.tensor_copy(x_codes[:], all_words[:].indirect(offs_sb[:]))
+        nc.vector.tensor_copy(x_plane[:], all_scales[:].indirect(offs_sb[:]))
+        for i in range(TILES):
+            quantise(i)
+            score(i)
+            if i > 0:
+                top(i - 1)
+        last = TILES - 1
+        top(last)
+        for i in range(last):
+            fetch(i)
+            sum_on_tensor(i)
+            if i > 0:
+                finish(i - 1)
+            nc.vector.tensor_reduce(best[i][:], gg[i][:], mybir.AxisListType.X, ALU.max)
+        fetch(last)
+        finish(last - 1)
+        max_pairs(last)
+        nc.vector.tensor_tensor(pair_sum[:], gg[last][:, :, 0:2], gg[last][:, :, 2:4], ALU.add)
+        max_final(last)
+        nc.vector.tensor_tensor(last_sum[:], pair_sum[:, :, 0], pair_sum[:, :, 1], ALU.add)
+        nc.vector.scalar_tensor_tensor(res[last][:], last_sum[:], 0.25 / D, best[last][:], ALU.mult, ALU.add)
+        store(last)

@@ -49,18 +49,22 @@ def tile_picked_yplaid_mix_p_kernel(tc, x_words, x_scales, hT, offs, code, out):
         y = tiles(psum, "y", [P, S], F32)
         u = tiles(sb, "u", [P, S], F32)
         bias = tiles(sb, "bias", [P, 1], F32)
-        tops = tiles(sb, "tops", [P, 1], F32)
-        gate = tiles(sb, "gate", [P, S], F32)
-        p = tiles(sb, "p", [P, S], F32)
+        top0 = sb.tile([P, 1], F32, name="top0")
+        window = tiles(sb, "window", [P, 2 * S], F32)
+        p = [w[:, :S] for w in window]
+        gate = [w[:, S:] for w in window]
         gg = tiles(sb, "gg", [P, PASSAGES, D], F32)
-        pair_max = {TILES - 1: sb.tile([P, PASSAGES, 2], F32, name="pair_max")}
+        pair_max = tiles(sb, "pair_max", [P, PASSAGES, 2], F32)
         best = tiles(sb, "best", [P, PASSAGES], F32)
         res = tiles(sb, "res", [P, PASSAGES], F32)
         mean_t = tiles(sb, "mean_t", [P, P], F32, count=TILES - 1)
+        best16 = tiles(sb, "best16", [P, PASSAGES], F32, count=TILES - 2)
         pair_sum = sb.tile([P, PASSAGES, 2], F32, name="pair_sum")
         last_sum = sb.tile([P, PASSAGES], F32, name="last_sum")
 
         nc.gpsimd.memset(all_scales[:].bitcast(I32), 0)
+        warm = sb.tile([P, 2], F32, name="warm")
+        nc.gpsimd.memset(warm[:, 0:1], 0.0)
         nc.sync.dma_start(offs_sb[:], offs)
         nc.sync.dma_start(all_words[:].bitcast(I32), x_words[0].rearrange("p n t -> p (n t)").bitcast(I32))
         for q in range(4):
@@ -68,6 +72,7 @@ def tile_picked_yplaid_mix_p_kernel(tc, x_words, x_scales, hT, offs, code, out):
                 all_scales[32 * q : 32 * q + 4, :].bitcast(I32),
                 x_scales[0, 4 * q : 4 * q + 4, :].bitcast(I32),
             )
+        nc.scalar.activation(warm[:, 1:2], warm[:, 0:1], ACT.Sigmoid)
         h_view = hT.rearrange("(p j) w -> p j w", j=PACK)
         for i in range(TILES):
             nc.sync.dma_start(h_raw[i][:], h_view[:, :, i * P : (i + 1) * P])
@@ -84,42 +89,45 @@ def tile_picked_yplaid_mix_p_kernel(tc, x_words, x_scales, hT, offs, code, out):
                 in_=h_bf[i][:].rearrange("p w j -> p (w j)"),
             )
 
-        def score(i):
+        def score(i, cols=slice(0, S)):
             nc.tensor.matmul_mx(
-                out=y[i][:],
+                out=y[i][:, cols],
                 lhsT=h_codes[i][:].bitcast(FP8X4),
                 lhsT_scale=h_plane[i][:],
-                rhs=x_codes[:].bitcast(FP8X4),
-                rhs_scale=x_plane[:],
+                rhs=x_codes[:, cols].bitcast(FP8X4),
+                rhs_scale=x_plane[:, cols],
                 start=True,
                 stop=True,
             )
 
         def top(i):
-            nc.vector.tensor_scalar(u[i][:], y[i][:], 1.0, None, ALU.mult, ALU.max, accum_out=tops[i][:])
-            nc.scalar.activation(bias[i][:], tops[i][:], ACT.Copy, scale=-2.4)
-            nc.scalar.activation(gate[i][:], u[i][:], ACT.Sigmoid, bias=bias[i][:], scale=6.0)
-            nc.gpsimd.tensor_tensor(p[i][:], u[i][:], gate[i][:], ALU.mult)
+            if i == 0:
+                nc.vector.tensor_scalar(u[i][:], y[i][:], 1.0, None, ALU.mult, ALU.max, accum_out=top0[:])
+                nc.scalar.activation(bias[i][:], top0[:], ACT.Copy, scale=-2.4)
+                nc.scalar.activation(gate[i], u[i][:], ACT.Sigmoid, bias=bias[i][:], scale=6.0)
+                nc.gpsimd.tensor_tensor(p[i], u[i][:], gate[i], ALU.mult)
+            else:
+                nc.vector.tensor_scalar(u[i][:], y[i][:], -2.4, None, ALU.mult, ALU.min, accum_out=bias[i][:])
+                nc.scalar.activation(gate[i], u[i][:], ACT.Sigmoid, bias=bias[i][:], scale=-2.5)
+
+        def fade(i):
+            nc.vector.tensor_tensor(p[i], y[i][:], gate[i], ALU.mult)
 
         def fetch(i):
-            flat = gg[i][:].rearrange("p v d -> p (v d)")
-            cols = HALF // LIST_ROWS
-            for h in range(2):
-                nc.vector.tensor_copy(
-                    flat[:, h * HALF : (h + 1) * HALF],
-                    p[i][:].indirect(code_sb[:, h * cols : (h + 1) * cols]),
-                )
+            nc.vector.tensor_copy(gg[i][:].rearrange("p v d -> p (v d)"), window[i][:].indirect(code_sb[:]))
 
-        mean = {}
-
-        def sum_on_tensor(i):
+        def sums_on_tensor(i, with_best):
             sum_t = psum.tile([P, P], F32, name="sum_t", bufs=2)
-            for d in range(D):
-                nc.tensor.matmul(sum_t[:], gg[i][:, :, d], ident[:], start=(d == 0), stop=(d == D - 1), is_transpose=True)
+            terms = [gg[i][:, :, d] for d in range(D)]
+            if with_best:
+                nc.scalar.activation(best16[i][:], best[i][:], ACT.Copy, scale=D / 0.25)
+                terms.append(best16[i][:])
+            for n, term in enumerate(terms):
+                nc.tensor.matmul(sum_t[:], term, ident[:], start=(n == 0), stop=(n == len(terms) - 1), is_transpose=True)
             nc.scalar.activation(mean_t[i][:], sum_t[:], ACT.Copy, scale=0.25 / D)
             back = psum.tile([P, P], F32, name="back", bufs=2)
             nc.tensor.transpose(back[:], mean_t[i][:], ident[:])
-            mean[i] = back
+            return back
 
         def max_pairs(i):
             nc.vector.tensor_tensor(pair_max[i][:], gg[i][:, :, 0:2], gg[i][:, :, 2:4], ALU.max)
@@ -130,30 +138,38 @@ def tile_picked_yplaid_mix_p_kernel(tc, x_words, x_scales, hT, offs, code, out):
         def store(i):
             nc.sync.dma_start(out[i * P : (i + 1) * P, :], res[i][:])
 
-        def finish(i):
-            nc.vector.tensor_tensor(res[i][:], mean[i][:], best[i][:], ALU.add)
-            store(i)
-
         for i in range(TILES):
             interleave(i)
         nc.vector.tensor_copy(x_codes[:], all_words[:].indirect(offs_sb[:]))
-        nc.vector.tensor_copy(x_plane[:], all_scales[:].indirect(offs_sb[:]))
-        for i in range(TILES):
+        for h in range(2):
+            cols = slice(h * S // 2, (h + 1) * S // 2)
+            entries = slice(cols.start // LIST_ROWS, cols.stop // LIST_ROWS)
+            nc.vector.tensor_copy(x_plane[:, cols], all_scales[:].indirect(offs_sb[:, entries]))
+            if h == 0:
+                quantise(0)
+            score(0, cols)
+        for i in range(1, TILES):
             quantise(i)
             score(i)
-            if i > 0:
-                top(i - 1)
+            top(i - 1)
         last = TILES - 1
         top(last)
-        for i in range(last):
-            fetch(i)
-            sum_on_tensor(i)
-            if i > 0:
-                finish(i - 1)
-            nc.vector.tensor_reduce(best[i][:], gg[i][:], mybir.AxisListType.X, ALU.max)
+        fade(1)
+        fetch(0)
+        for i in range(TILES - 2):
+            fade(i + 2)
+            max_pairs(i)
+            fetch(i + 1)
+            max_final(i)
+            nc.scalar.copy(res[i][:], sums_on_tensor(i, True)[:])
+            store(i)
+        mean = sums_on_tensor(last - 1, False)
+        max_pairs(last - 1)
         fetch(last)
-        finish(last - 1)
+        max_final(last - 1)
         max_pairs(last)
+        nc.vector.tensor_tensor(res[last - 1][:], mean[:], best[last - 1][:], ALU.add)
+        store(last - 1)
         nc.vector.tensor_tensor(pair_sum[:], gg[last][:, :, 0:2], gg[last][:, :, 2:4], ALU.add)
         max_final(last)
         nc.vector.tensor_tensor(last_sum[:], pair_sum[:, :, 0], pair_sum[:, :, 1], ALU.add)

@@ -49,12 +49,11 @@ def tile_picked_yplaid_mix_p_kernel(tc, x_words, x_scales, hT, offs, code, out):
         y = tiles(psum, "y", [P, S], F32)
         u = tiles(sb, "u", [P, S], F32)
         bias = tiles(sb, "bias", [P, 1], F32)
-        top0 = sb.tile([P, 1], F32, name="top0")
-        window = tiles(sb, "window", [P, 2 * S], F32)
-        p = [w[:, :S] for w in window]
-        gate = [w[:, S:] for w in window]
+        tops = tiles(sb, "tops", [P, 1], F32)
+        gate = tiles(sb, "gate", [P, S], F32)
+        p = tiles(sb, "p", [P, S], F32)
         gg = tiles(sb, "gg", [P, PASSAGES, D], F32)
-        pair_max = tiles(sb, "pair_max", [P, PASSAGES, 2], F32)
+        pair_max = sb.tile([P, PASSAGES, 2], F32, name="pair_max")
         best = tiles(sb, "best", [P, PASSAGES], F32)
         res = tiles(sb, "res", [P, PASSAGES], F32)
         mean_t = tiles(sb, "mean_t", [P, P], F32, count=TILES - 1)
@@ -80,7 +79,11 @@ def tile_picked_yplaid_mix_p_kernel(tc, x_words, x_scales, hT, offs, code, out):
         make_identity(nc, ident[:])
 
         def interleave(i):
-            nc.scalar.copy(h_bf[i][:], h_raw[i][:].rearrange("p j w -> p w j"))
+            src = h_raw[i][:].rearrange("p j w -> p w j")
+            if i < TILES - 1:
+                nc.scalar.copy(h_bf[i][:], src)
+            else:
+                nc.gpsimd.tensor_scalar(h_bf[i][:], src, 1.0, 0.0, ALU.mult, ALU.add)
 
         def quantise(i):
             nc.vector.quantize_mx(
@@ -101,20 +104,17 @@ def tile_picked_yplaid_mix_p_kernel(tc, x_words, x_scales, hT, offs, code, out):
             )
 
         def top(i):
-            if i == 0:
-                nc.vector.tensor_scalar(u[i][:], y[i][:], 1.0, None, ALU.mult, ALU.max, accum_out=top0[:])
-                nc.scalar.activation(bias[i][:], top0[:], ACT.Copy, scale=-2.4)
-                nc.scalar.activation(gate[i], u[i][:], ACT.Sigmoid, bias=bias[i][:], scale=6.0)
-                nc.gpsimd.tensor_tensor(p[i], u[i][:], gate[i], ALU.mult)
-            else:
-                nc.vector.tensor_scalar(u[i][:], y[i][:], -2.4, None, ALU.mult, ALU.min, accum_out=bias[i][:])
-                nc.scalar.activation(gate[i], u[i][:], ACT.Sigmoid, bias=bias[i][:], scale=-2.5)
+            nc.vector.tensor_scalar(u[i][:], y[i][:], 1.0, None, ALU.mult, ALU.max, accum_out=tops[i][:])
+            nc.scalar.activation(bias[i][:], tops[i][:], ACT.Copy, scale=-2.4)
+            nc.scalar.activation(gate[i][:], u[i][:], ACT.Sigmoid, bias=bias[i][:], scale=6.0)
+            nc.gpsimd.tensor_tensor(p[i][:], u[i][:], gate[i][:], ALU.mult)
 
-        def fade(i):
-            nc.vector.tensor_tensor(p[i], y[i][:], gate[i], ALU.mult)
+        halves = [slice(h * PASSAGES // 2, (h + 1) * PASSAGES // 2) for h in range(2)]
 
         def fetch(i):
-            nc.vector.tensor_copy(gg[i][:].rearrange("p v d -> p (v d)"), window[i][:].indirect(code_sb[:]))
+            for half in halves:
+                entries = code_sb[:, half.start * D // LIST_ROWS : half.stop * D // LIST_ROWS]
+                nc.vector.tensor_copy(gg[i][:, half, :].rearrange("p v d -> p (v d)"), p[i][:].indirect(entries))
 
         def sums_on_tensor(i, with_best):
             sum_t = psum.tile([P, P], F32, name="sum_t", bufs=2)
@@ -129,49 +129,35 @@ def tile_picked_yplaid_mix_p_kernel(tc, x_words, x_scales, hT, offs, code, out):
             nc.tensor.transpose(back[:], mean_t[i][:], ident[:])
             return back
 
-        def max_pairs(i):
-            nc.vector.tensor_tensor(pair_max[i][:], gg[i][:, :, 0:2], gg[i][:, :, 2:4], ALU.max)
-
-        def max_final(i):
-            nc.vector.tensor_tensor(best[i][:], pair_max[i][:, :, 0], pair_max[i][:, :, 1], ALU.max)
-
         def store(i):
             nc.sync.dma_start(out[i * P : (i + 1) * P, :], res[i][:])
 
         for i in range(TILES):
             interleave(i)
         nc.vector.tensor_copy(x_codes[:], all_words[:].indirect(offs_sb[:]))
-        for h in range(2):
-            cols = slice(h * S // 2, (h + 1) * S // 2)
-            entries = slice(cols.start // LIST_ROWS, cols.stop // LIST_ROWS)
-            nc.vector.tensor_copy(x_plane[:, cols], all_scales[:].indirect(offs_sb[:, entries]))
-            if h == 0:
-                quantise(0)
-            score(0, cols)
-        for i in range(1, TILES):
+        nc.vector.tensor_copy(x_plane[:], all_scales[:].indirect(offs_sb[:]))
+        for i in range(TILES):
             quantise(i)
             score(i)
-            top(i - 1)
+            if i > 0:
+                top(i - 1)
         last = TILES - 1
         top(last)
-        fade(1)
-        fetch(0)
-        for i in range(TILES - 2):
-            fade(i + 2)
-            max_pairs(i)
-            fetch(i + 1)
-            max_final(i)
-            nc.scalar.copy(res[i][:], sums_on_tensor(i, True)[:])
-            store(i)
+        for i in range(last):
+            fetch(i)
+            for half in halves:
+                nc.vector.tensor_reduce(best[i][:, half], gg[i][:, half, :], mybir.AxisListType.X, ALU.max)
+            if i < last - 1:
+                nc.scalar.copy(res[i][:], sums_on_tensor(i, True)[:])
+                store(i)
         mean = sums_on_tensor(last - 1, False)
-        max_pairs(last - 1)
         fetch(last)
-        max_final(last - 1)
-        max_pairs(last)
+        for half in halves:
+            nc.vector.tensor_tensor(pair_max[:, half, :], gg[last][:, half, 0:2], gg[last][:, half, 2:4], ALU.max)
+            nc.vector.tensor_tensor(pair_sum[:, half, :], gg[last][:, half, 0:2], gg[last][:, half, 2:4], ALU.add)
+        nc.vector.tensor_tensor(best[last][:], pair_max[:, :, 0], pair_max[:, :, 1], ALU.max)
+        nc.vector.tensor_tensor(last_sum[:], pair_sum[:, :, 0], pair_sum[:, :, 1], ALU.add)
         nc.vector.tensor_tensor(res[last - 1][:], mean[:], best[last - 1][:], ALU.add)
         store(last - 1)
-        nc.vector.tensor_tensor(pair_sum[:], gg[last][:, :, 0:2], gg[last][:, :, 2:4], ALU.add)
-        max_final(last)
-        nc.vector.tensor_tensor(last_sum[:], pair_sum[:, :, 0], pair_sum[:, :, 1], ALU.add)
         nc.vector.scalar_tensor_tensor(res[last][:], last_sum[:], 0.25 / D, best[last][:], ALU.mult, ALU.add)
         store(last)

@@ -15,13 +15,16 @@ U8 = mybir.dt.uint8
 FP8X4 = mybir.dt.float8_e4m3fn_x4
 ALU = mybir.AluOpType
 ACT = mybir.ActivationFunctionType
+AXIS_X = mybir.AxisListType.X
 
 P = 128
 PACK = 4
 TILES = V // P
 PASSAGES = U // D
-HALF = U // 2
 LIST_ROWS = 16
+SLOPE = 6.0
+CUT = 0.4
+MEAN_WEIGHT = 0.25 / D
 
 
 def tile_picked_yplaid_mix_p_kernel(tc, x_words, x_scales, hT, offs, code, out):
@@ -31,6 +34,9 @@ def tile_picked_yplaid_mix_p_kernel(tc, x_words, x_scales, hT, offs, code, out):
         sb = ctx.enter_context(tc.tile_pool(name="sb", bufs=1))
         psum = ctx.enter_context(tc.psum_pool(name="psum", bufs=1))
 
+        def tiles(pool, stem, shape, dtype, count=TILES, **kw):
+            return [pool.tile(shape, dtype, name=f"{stem}{i}", **kw) for i in range(count)]
+
         offs_sb = lists.tile([P, S // LIST_ROWS], U16, name="offs_sb")
         code_sb = lists.tile([P, U // LIST_ROWS], U16, name="code_sb")
         all_words = sb.tile([P, T], U32, name="all_words")
@@ -38,126 +44,176 @@ def tile_picked_yplaid_mix_p_kernel(tc, x_words, x_scales, hT, offs, code, out):
         x_codes = sb.tile([P, S], U32, name="x_codes", align_bytes=64)
         x_plane = sb.tile([P, S], U8, name="x_plane", align_bytes=64)
         ident = sb.tile([P, P], F32, name="ident")
-
-        def tiles(pool, stem, shape, dtype, count=TILES, **kw):
-            return [pool.tile(shape, dtype, name=f"{stem}{i}", **kw) for i in range(count)]
-
-        h_raw = tiles(sb, "h_raw", [P, PACK, P], F32)
-        h_bf = tiles(sb, "h_bf", [P, P, PACK], BF16, align_bytes=64)
-        h_codes = tiles(sb, "h_codes", [P, P], U32, align_bytes=64)
-        h_plane = tiles(sb, "h_plane", [P, P], U8, align_bytes=64)
+        warm = sb.tile([P, 2], F32, name="warm")
+        u = [t[:] for t in tiles(sb, "u", [P, S], F32, align_bytes=64)]
+        first_bf = sb.tile([P, PACK * P], BF16, name="first_bf", align_bytes=64)
+        late_bf = u[1].bitcast(BF16)
+        early_raw = tiles(sb, "early_raw", [P, PACK, P], F32, count=2)
+        late_raw = sb.tile([P, PACK, 2 * P], F32, name="late_raw")
+        gate = [late_raw[:].rearrange("p j w -> p (j w)")[:, :S]]
+        gate = gate + [t[:] for t in tiles(sb, "gate", [P, S], F32, count=TILES - 1)]
+        h_raw = [early_raw[0][:], early_raw[1][:], late_raw[:, :, :P], late_raw[:, :, P:]]
+        h_bf = [first_bf[:], u[0][:, : PACK * P // 2].bitcast(BF16), late_bf[:, : PACK * P], late_bf[:, PACK * P :]]
+        h_codes = sb.tile([P, V], U32, name="h_codes", align_bytes=64)
+        h_plane = sb.tile([P, V], U8, name="h_plane", align_bytes=64)
         y = tiles(psum, "y", [P, S], F32)
-        u = tiles(sb, "u", [P, S], F32)
-        bias = tiles(sb, "bias", [P, 1], F32)
         tops = tiles(sb, "tops", [P, 1], F32)
-        gate = tiles(sb, "gate", [P, S], F32)
-        p = tiles(sb, "p", [P, S], F32)
+        bias = tiles(sb, "bias", [P, 1], F32)
+        p = [t[:] for t in tiles(sb, "p", [P, S], F32)]
+        wide = sb.tile([P, 2 * S], F32, name="wide")
+        p[1] = wide[:, :S]
+        gate[1] = wide[:, S:]
         gg = tiles(sb, "gg", [P, PASSAGES, D], F32)
-        pair_max = sb.tile([P, PASSAGES, 2], F32, name="pair_max")
-        best = tiles(sb, "best", [P, PASSAGES], F32)
-        res = tiles(sb, "res", [P, PASSAGES], F32)
-        mean_t = tiles(sb, "mean_t", [P, P], F32, count=TILES - 1)
-        best16 = tiles(sb, "best16", [P, PASSAGES], F32, count=TILES - 2)
-        pair_sum = sb.tile([P, PASSAGES, 2], F32, name="pair_sum")
-        last_sum = sb.tile([P, PASSAGES], F32, name="last_sum")
+        best_all = sb.tile([P, TILES, PASSAGES], F32, name="best_all")
+        res_all = sb.tile([P, TILES, PASSAGES], F32, name="res_all")
+        best = [best_all[:, i, :] for i in range(TILES)]
+        res = [res_all[:, i, :] for i in range(TILES)]
+        out_view = out.rearrange("(i p) v -> p i v", p=P)
 
         nc.gpsimd.memset(all_scales[:].bitcast(I32), 0)
-        warm = sb.tile([P, 2], F32, name="warm")
         nc.gpsimd.memset(warm[:, 0:1], 0.0)
+        h_view = hT.rearrange("(p j) w -> p j w", j=PACK)
         nc.sync.dma_start(offs_sb[:], offs)
-        nc.sync.dma_start(all_words[:].bitcast(I32), x_words[0].rearrange("p n t -> p (n t)").bitcast(I32))
         for q in range(4):
-            nc.sync.dma_start(
+            (nc.sync if q < 2 else nc.scalar).dma_start(
                 all_scales[32 * q : 32 * q + 4, :].bitcast(I32),
                 x_scales[0, 4 * q : 4 * q + 4, :].bitcast(I32),
             )
-        nc.scalar.activation(warm[:, 1:2], warm[:, 0:1], ACT.Sigmoid)
-        h_view = hT.rearrange("(p j) w -> p j w", j=PACK)
-        for i in range(TILES):
-            nc.sync.dma_start(h_raw[i][:], h_view[:, :, i * P : (i + 1) * P])
+        nc.sync.dma_start(all_words[:].bitcast(I32), x_words[0].rearrange("p n t -> p (n t)").bitcast(I32))
+        nc.sync.dma_start(h_raw[0], h_view[:, :, 0 * P : 1 * P])
+        nc.sync.dma_start(h_raw[1], h_view[:, :, 1 * P : 2 * P])
+        nc.sync.dma_start(late_raw[:], h_view[:, :, 2 * P :])
         nc.sync.dma_start(code_sb[:], code)
+        nc.scalar.activation(warm[:, 1:2], warm[:, 0:1], ACT.Sigmoid)
         make_identity(nc, ident[:])
 
-        def interleave(i):
-            src = h_raw[i][:].rearrange("p j w -> p w j")
-            if i < TILES - 1:
-                nc.scalar.copy(h_bf[i][:], src)
-            else:
-                nc.gpsimd.tensor_scalar(h_bf[i][:], src, 1.0, 0.0, ALU.mult, ALU.add)
+        def round_on_scalar(i):
+            nc.scalar.copy(h_bf[i].rearrange("p (w j) -> p w j", j=PACK), h_raw[i].rearrange("p j w -> p w j"))
 
-        def quantise(i):
-            nc.vector.quantize_mx(
-                out=h_codes[i][:].bitcast(FP8X4),
-                scales=h_plane[i][:],
-                in_=h_bf[i][:].rearrange("p w j -> p (w j)"),
-            )
+        def round_on_gpsimd(i):
+            nc.gpsimd.tensor_scalar(h_bf[i].rearrange("p (w j) -> p w j", j=PACK), h_raw[i].rearrange("p j w -> p w j"), 1.0, 0.0, ALU.mult, ALU.add)
 
-        def score(i, cols=slice(0, S)):
+        def quantise(tokens, src):
+            nc.vector.quantize_mx(out=h_codes[:, tokens].bitcast(FP8X4), scales=h_plane[:, tokens], in_=src)
+
+        def score(i):
             nc.tensor.matmul_mx(
-                out=y[i][:, cols],
-                lhsT=h_codes[i][:].bitcast(FP8X4),
-                lhsT_scale=h_plane[i][:],
-                rhs=x_codes[:, cols].bitcast(FP8X4),
-                rhs_scale=x_plane[:, cols],
+                out=y[i][:],
+                lhsT=h_codes[:, i * P : (i + 1) * P].bitcast(FP8X4),
+                lhsT_scale=h_plane[:, i * P : (i + 1) * P],
+                rhs=x_codes[:].bitcast(FP8X4),
+                rhs_scale=x_plane[:],
                 start=True,
                 stop=True,
             )
 
-        def top(i):
-            nc.vector.tensor_scalar(u[i][:], y[i][:], 1.0, None, ALU.mult, ALU.max, accum_out=tops[i][:])
-            nc.scalar.activation(bias[i][:], tops[i][:], ACT.Copy, scale=-2.4)
-            nc.scalar.activation(gate[i][:], u[i][:], ACT.Sigmoid, bias=bias[i][:], scale=6.0)
-            nc.gpsimd.tensor_tensor(p[i][:], u[i][:], gate[i][:], ALU.mult)
+        def gate_keeping_y(i):
+            nc.vector.tensor_scalar(u[i], y[i][:], 1.0, None, ALU.mult, ALU.max, accum_out=tops[i][:])
+            nc.scalar.activation(bias[i][:], tops[i][:], ACT.Copy, scale=-SLOPE * CUT)
+            nc.scalar.activation(gate[i], u[i], ACT.Sigmoid, bias=bias[i][:], scale=SLOPE)
+
+        def gate_from_scaled_y(i):
+            nc.vector.tensor_scalar(u[i], y[i][:], -SLOPE * CUT, None, ALU.mult, ALU.min, accum_out=bias[i][:])
+            nc.scalar.activation(gate[i], u[i], ACT.Sigmoid, bias=bias[i][:], scale=-1.0 / CUT)
+
+        def fade_on_gpsimd(i, cols=slice(0, S)):
+            nc.gpsimd.tensor_tensor(p[i][:, cols], u[i][:, cols], gate[i][:, cols], ALU.mult)
+
+        def fade_on_vector(i, cols=slice(0, S)):
+            nc.vector.tensor_tensor(p[i][:, cols], y[i][:, cols], gate[i][:, cols], ALU.mult)
 
         halves = [slice(h * PASSAGES // 2, (h + 1) * PASSAGES // 2) for h in range(2)]
 
-        def fetch(i):
-            for half in halves:
-                entries = code_sb[:, half.start * D // LIST_ROWS : half.stop * D // LIST_ROWS]
-                nc.vector.tensor_copy(gg[i][:, half, :].rearrange("p v d -> p (v d)"), p[i][:].indirect(entries))
+        def window(i, h):
+            half = halves[h]
+            entries = code_sb[:, half.start * D // LIST_ROWS : half.stop * D // LIST_ROWS]
+            return gg[i][:, half, :].rearrange("p v d -> p (v d)"), p[i].indirect(entries)
 
-        def sums_on_tensor(i, with_best):
-            sum_t = psum.tile([P, P], F32, name="sum_t", bufs=2)
-            terms = [gg[i][:, :, d] for d in range(D)]
-            if with_best:
-                nc.scalar.activation(best16[i][:], best[i][:], ACT.Copy, scale=D / 0.25)
-                terms.append(best16[i][:])
-            for n, term in enumerate(terms):
-                nc.tensor.matmul(sum_t[:], term, ident[:], start=(n == 0), stop=(n == len(terms) - 1), is_transpose=True)
-            nc.scalar.activation(mean_t[i][:], sum_t[:], ACT.Copy, scale=0.25 / D)
-            back = psum.tile([P, P], F32, name="back", bufs=2)
-            nc.tensor.transpose(back[:], mean_t[i][:], ident[:])
+        def fetch_on_vector(i, h):
+            nc.vector.tensor_copy(*window(i, h))
+
+        def fetch_on_scalar(i, h):
+            nc.scalar.activation(*window(i, h), ACT.Copy)
+
+        def largest(i, h):
+            nc.vector.tensor_reduce(best[i][:, halves[h]], gg[i][:, halves[h], :], AXIS_X, ALU.max)
+
+        def means_on_tensor(first, count):
+            sum_t = psum.tile([P, count, P], F32, name=f"sum_t{first}")
+            for n in range(count):
+                for d in range(D):
+                    nc.tensor.matmul(
+                        sum_t[:, n, :], gg[first + n][:, :, d], ident[:], start=(d == 0), stop=(d == D - 1), is_transpose=True
+                    )
+            mean_t = sb.tile([P, count, P], F32, name=f"mean_t{first}")
+            nc.scalar.activation(mean_t[:], sum_t[:], ACT.Copy, scale=MEAN_WEIGHT)
+            back = psum.tile([P, count, P], F32, name=f"back{first}")
+            for n in range(count):
+                nc.tensor.transpose(back[:, n, :], mean_t[:, n, :], ident[:])
             return back
 
-        def store(i):
-            nc.sync.dma_start(out[i * P : (i + 1) * P, :], res[i][:])
+        def finish(first, count, back):
+            rows = slice(first, first + count)
+            nc.vector.tensor_tensor(res_all[:, rows, :], back[:], best_all[:, rows, :], ALU.add)
+            nc.sync.dma_start(out_view[:, rows, :], res_all[:, rows, :])
 
-        for i in range(TILES):
-            interleave(i)
-        nc.vector.tensor_copy(x_codes[:], all_words[:].indirect(offs_sb[:]))
+        pair_max = sb.tile([P, PASSAGES, 2], F32, name="pair_max")
+        pair_sum = sb.tile([P, PASSAGES, 2], F32, name="pair_sum")
+        last_sum = sb.tile([P, PASSAGES], F32, name="last_sum")
+
+        def pairs(i, h):
+            half = halves[h]
+            nc.vector.tensor_tensor(pair_max[:, half, :], gg[i][:, half, 0:2], gg[i][:, half, 2:4], ALU.max)
+            nc.vector.tensor_tensor(pair_sum[:, half, :], gg[i][:, half, 0:2], gg[i][:, half, 2:4], ALU.add)
+
+        def finish_pairs(i):
+            nc.vector.tensor_tensor(best[i], pair_max[:, :, 0], pair_max[:, :, 1], ALU.max)
+            nc.vector.tensor_tensor(last_sum[:], pair_sum[:, :, 0], pair_sum[:, :, 1], ALU.add)
+            nc.vector.scalar_tensor_tensor(res[i], last_sum[:], MEAN_WEIGHT, best[i], ALU.mult, ALU.add)
+            nc.sync.dma_start(out[i * P : (i + 1) * P, :], res[i])
+
+        def fetch_whole_on_scalar(i):
+            nc.scalar.activation(gg[i][:].rearrange("p v d -> p (v d)"), wide[:].indirect(code_sb[:]), ACT.Copy)
+
+        def largest_whole(i):
+            nc.vector.tensor_reduce(best[i], gg[i][:], AXIS_X, ALU.max)
+
+        round_on_scalar(0)
+        round_on_scalar(1)
+        round_on_scalar(2)
+        round_on_gpsimd(3)
         nc.vector.tensor_copy(x_plane[:], all_scales[:].indirect(offs_sb[:]))
-        for i in range(TILES):
-            quantise(i)
-            score(i)
-            if i > 0:
-                top(i - 1)
-        last = TILES - 1
-        top(last)
-        for i in range(last):
-            fetch(i)
-            for half in halves:
-                nc.vector.tensor_reduce(best[i][:, half], gg[i][:, half, :], mybir.AxisListType.X, ALU.max)
-            if i < last - 1:
-                nc.scalar.copy(res[i][:], sums_on_tensor(i, True)[:])
-                store(i)
-        mean = sums_on_tensor(last - 1, False)
-        fetch(last)
-        for half in halves:
-            nc.vector.tensor_tensor(pair_max[:, half, :], gg[last][:, half, 0:2], gg[last][:, half, 2:4], ALU.max)
-            nc.vector.tensor_tensor(pair_sum[:, half, :], gg[last][:, half, 0:2], gg[last][:, half, 2:4], ALU.add)
-        nc.vector.tensor_tensor(best[last][:], pair_max[:, :, 0], pair_max[:, :, 1], ALU.max)
-        nc.vector.tensor_tensor(last_sum[:], pair_sum[:, :, 0], pair_sum[:, :, 1], ALU.add)
-        nc.vector.tensor_tensor(res[last - 1][:], mean[:], best[last - 1][:], ALU.add)
-        store(last - 1)
-        nc.vector.scalar_tensor_tensor(res[last][:], last_sum[:], 0.25 / D, best[last][:], ALU.mult, ALU.add)
-        store(last)
+        nc.vector.tensor_copy(x_codes[:], all_words[:].indirect(offs_sb[:]))
+        quantise(slice(0, P), h_bf[0])
+        score(0)
+        quantise(slice(P, 2 * P), h_bf[1])
+        score(1)
+        gate_keeping_y(0)
+        quantise(slice(2 * P, V), late_bf)
+        score(2)
+        score(3)
+        fade_on_gpsimd(0)
+        gate_keeping_y(1)
+        fade_on_gpsimd(1)
+        gate_from_scaled_y(2)
+        gate_keeping_y(3)
+        fade_on_gpsimd(3)
+        fetch_on_vector(0, 0)
+        fetch_on_scalar(0, 1)
+        fade_on_vector(2)
+        largest(0, 0)
+        largest(0, 1)
+        fetch_whole_on_scalar(1)
+        back0 = means_on_tensor(0, 1)
+        fetch_on_vector(2, 0)
+        fetch_on_vector(2, 1)
+        largest_whole(1)
+        finish(0, 1, back0)
+        fetch_on_scalar(3, 0)
+        fetch_on_scalar(3, 1)
+        back1 = means_on_tensor(1, 2)
+        largest_whole(2)
+        pairs(3, 0)
+        pairs(3, 1)
+        finish(1, 2, back1)
+        finish_pairs(3)

@@ -57,13 +57,10 @@ def tile_picked_yplaid_mix_p_kernel(tc, x_words, x_scales, hT, offs, code, out):
         h_codes = sb.tile([P, V], U32, name="h_codes", align_bytes=64)
         h_plane = sb.tile([P, V], U8, name="h_plane", align_bytes=64)
         y = tiles(psum, "y", [P, S], F32)
-        tops = tiles(sb, "tops", [P, 1], F32)
         bias = tiles(sb, "bias", [P, 1], F32)
         p = [t[:] for t in tiles(sb, "p", [P, S], F32)]
-        wide = sb.tile([P, 2 * S], F32, name="wide")
-        p[1] = wide[:, :S]
-        gate[1] = wide[:, S:]
         gg = tiles(sb, "gg", [P, PASSAGES, D], F32)
+        tops = [t[:] for t in tiles(sb, "tops", [P, 1], F32, count=TILES - 1)] + [gg[0][:, PASSAGES - 1, D - 1 :]]
         best_all = sb.tile([P, TILES, PASSAGES], F32, name="best_all")
         res_all = sb.tile([P, TILES, PASSAGES], F32, name="res_all")
         best = [best_all[:, i, :] for i in range(TILES)]
@@ -107,10 +104,11 @@ def tile_picked_yplaid_mix_p_kernel(tc, x_words, x_scales, hT, offs, code, out):
                 stop=True,
             )
 
-        def gate_keeping_y(i):
-            nc.vector.tensor_scalar(u[i], y[i][:], 1.0, None, ALU.mult, ALU.max, accum_out=tops[i][:])
-            nc.scalar.activation(bias[i][:], tops[i][:], ACT.Copy, scale=-SLOPE * CUT)
-            nc.scalar.activation(gate[i], u[i], ACT.Sigmoid, bias=bias[i][:], scale=SLOPE)
+        def gate_keeping_y(i, parts=(slice(0, S),)):
+            nc.vector.tensor_scalar(u[i], y[i][:], 1.0, None, ALU.mult, ALU.max, accum_out=tops[i])
+            nc.scalar.activation(bias[i][:], tops[i], ACT.Copy, scale=-SLOPE * CUT)
+            for cols in parts:
+                nc.scalar.activation(gate[i][:, cols], u[i][:, cols], ACT.Sigmoid, bias=bias[i][:], scale=SLOPE)
 
         def gate_from_scaled_y(i):
             nc.vector.tensor_scalar(u[i], y[i][:], -SLOPE * CUT, None, ALU.mult, ALU.min, accum_out=bias[i][:])
@@ -157,27 +155,25 @@ def tile_picked_yplaid_mix_p_kernel(tc, x_words, x_scales, hT, offs, code, out):
             nc.vector.tensor_tensor(res_all[:, rows, :], back[:], best_all[:, rows, :], ALU.add)
             nc.sync.dma_start(out_view[:, rows, :], res_all[:, rows, :])
 
-        pair_max = sb.tile([P, PASSAGES, 2], F32, name="pair_max")
         pair_sum = sb.tile([P, PASSAGES, 2], F32, name="pair_sum")
-        last_sum = sb.tile([P, PASSAGES], F32, name="last_sum")
-
-        def pairs(i, h):
-            half = halves[h]
-            nc.vector.tensor_tensor(pair_max[:, half, :], gg[i][:, half, 0:2], gg[i][:, half, 2:4], ALU.max)
-            nc.vector.tensor_tensor(pair_sum[:, half, :], gg[i][:, half, 0:2], gg[i][:, half, 2:4], ALU.add)
-
-        def finish_pairs(i):
-            nc.vector.tensor_tensor(best[i], pair_max[:, :, 0], pair_max[:, :, 1], ALU.max)
-            nc.vector.tensor_tensor(last_sum[:], pair_sum[:, :, 0], pair_sum[:, :, 1], ALU.add)
-            nc.vector.scalar_tensor_tensor(res[i], last_sum[:], MEAN_WEIGHT, best[i], ALU.mult, ALU.add)
-            nc.sync.dma_start(out[i * P : (i + 1) * P, :], res[i])
-
-        def fetch_whole_on_scalar(i):
-            nc.scalar.activation(gg[i][:].rearrange("p v d -> p (v d)"), wide[:].indirect(code_sb[:]), ACT.Copy)
+        late_sum = sb.tile([P, 2, PASSAGES], F32, name="late_sum")
 
         def largest_whole(i):
             nc.vector.tensor_reduce(best[i], gg[i][:], AXIS_X, ALU.max)
 
+        def sums_on_gpsimd(i, h):
+            half = halves[h]
+            nc.gpsimd.tensor_tensor(pair_sum[:, half, :], gg[i][:, half, 0:2], gg[i][:, half, 2:4], ALU.add)
+            nc.gpsimd.tensor_tensor(late_sum[:, i - 2, half], pair_sum[:, half, 0], pair_sum[:, half, 1], ALU.add)
+
+        def finish_from_sums(i):
+            nc.vector.scalar_tensor_tensor(res[i], late_sum[:, i - 2, :], MEAN_WEIGHT, best[i], ALU.mult, ALU.add)
+            nc.sync.dma_start(out[i * P : (i + 1) * P, :], res[i])
+
+        def sums_on_vector(i, h):
+            nc.vector.tensor_reduce(late_sum[:, i - 2, halves[h]], gg[i][:, halves[h], :], AXIS_X, ALU.add)
+
+        column_halves = (slice(0, S // 2), slice(S // 2, S))
         round_on_scalar(0)
         round_on_scalar(1)
         round_on_scalar(2)
@@ -188,11 +184,12 @@ def tile_picked_yplaid_mix_p_kernel(tc, x_words, x_scales, hT, offs, code, out):
         score(0)
         quantise(slice(P, 2 * P), h_bf[1])
         score(1)
-        gate_keeping_y(0)
+        gate_keeping_y(0, column_halves)
         quantise(slice(2 * P, V), late_bf)
         score(2)
         score(3)
-        fade_on_gpsimd(0)
+        for cols in column_halves:
+            fade_on_gpsimd(0, cols)
         gate_keeping_y(1)
         fade_on_gpsimd(1)
         gate_from_scaled_y(2)
@@ -202,18 +199,24 @@ def tile_picked_yplaid_mix_p_kernel(tc, x_words, x_scales, hT, offs, code, out):
         fetch_on_scalar(0, 1)
         fade_on_vector(2)
         largest(0, 0)
+        fetch_on_vector(1, 0)
+        fetch_on_scalar(1, 1)
         largest(0, 1)
-        fetch_whole_on_scalar(1)
+        fetch_on_scalar(2, 1)
         back0 = means_on_tensor(0, 1)
         fetch_on_vector(2, 0)
-        fetch_on_vector(2, 1)
+        sums_on_gpsimd(2, 1)
+        sums_on_gpsimd(2, 0)
+        fetch_on_scalar(3, 0)
+        back1 = means_on_tensor(1, 1)
+        fetch_on_scalar(3, 1)
         largest_whole(1)
         finish(0, 1, back0)
-        fetch_on_scalar(3, 0)
-        fetch_on_scalar(3, 1)
-        back1 = means_on_tensor(1, 2)
         largest_whole(2)
-        pairs(3, 0)
-        pairs(3, 1)
-        finish(1, 2, back1)
-        finish_pairs(3)
+        largest(3, 0)
+        sums_on_vector(3, 0)
+        finish(1, 1, back1)
+        largest(3, 1)
+        sums_on_vector(3, 1)
+        finish_from_sums(2)
+        finish_from_sums(3)

@@ -211,12 +211,12 @@ def tile_picked_yplaid_mix_p_kernel(tc, x_words, x_scales, hT, offs, code, out):
         back1 = means_on_tensor(1, 1)
         fetch_on_scalar(3, 1)
         largest_whole(1)
-        finish(0, 1, back0)
         largest_whole(2)
+        finish(0, 1, back0)
         largest(3, 0)
         sums_on_vector(3, 0)
-        finish(1, 1, back1)
         largest(3, 1)
         sums_on_vector(3, 1)
         finish_from_sums(2)
+        finish(1, 1, back1)
         finish_from_sums(3)

@@ -164,14 +164,14 @@ def tile_picked_yplaid_mix_p_kernel(tc, x_words, x_scales, hT, offs, code, out):
         def sums_on_gpsimd(i, h):
             half = halves[h]
             nc.gpsimd.tensor_tensor(pair_sum[:, half, :], gg[i][:, half, 0:2], gg[i][:, half, 2:4], ALU.add)
-            nc.gpsimd.tensor_tensor(late_sum[:, i - 2, half], pair_sum[:, half, 0], pair_sum[:, half, 1], ALU.add)
+            nc.gpsimd.tensor_tensor(late_sum[:, i // 2, half], pair_sum[:, half, 0], pair_sum[:, half, 1], ALU.add)
 
         def finish_from_sums(i):
-            nc.vector.scalar_tensor_tensor(res[i], late_sum[:, i - 2, :], MEAN_WEIGHT, best[i], ALU.mult, ALU.add)
+            nc.vector.scalar_tensor_tensor(res[i], late_sum[:, i // 2, :], MEAN_WEIGHT, best[i], ALU.mult, ALU.add)
             nc.sync.dma_start(out[i * P : (i + 1) * P, :], res[i])
 
         def sums_on_vector(i, h):
-            nc.vector.tensor_reduce(late_sum[:, i - 2, halves[h]], gg[i][:, halves[h], :], AXIS_X, ALU.add)
+            nc.vector.tensor_reduce(late_sum[:, i // 2, halves[h]], gg[i][:, halves[h], :], AXIS_X, ALU.add)
 
         column_halves = (slice(0, S // 2), slice(S // 2, S))
         round_on_scalar(0)
@@ -199,24 +199,24 @@ def tile_picked_yplaid_mix_p_kernel(tc, x_words, x_scales, hT, offs, code, out):
         fetch_on_scalar(0, 1)
         fade_on_vector(2)
         largest(0, 0)
-        fetch_on_vector(1, 0)
+        fetch_on_vector(2, 0)
         fetch_on_scalar(1, 1)
         largest(0, 1)
         fetch_on_scalar(2, 1)
         back0 = means_on_tensor(0, 1)
-        fetch_on_vector(2, 0)
-        sums_on_gpsimd(2, 1)
-        sums_on_gpsimd(2, 0)
+        fetch_on_vector(1, 0)
+        sums_on_gpsimd(1, 1)
+        sums_on_gpsimd(1, 0)
         fetch_on_scalar(3, 0)
-        back1 = means_on_tensor(1, 1)
+        back2 = means_on_tensor(2, 1)
         fetch_on_scalar(3, 1)
-        largest_whole(1)
         largest_whole(2)
+        largest_whole(1)
         finish(0, 1, back0)
         largest(3, 0)
         sums_on_vector(3, 0)
         largest(3, 1)
         sums_on_vector(3, 1)
-        finish_from_sums(2)
-        finish(1, 1, back1)
+        finish_from_sums(1)
+        finish(2, 1, back2)
         finish_from_sums(3)

@@ -22,6 +22,8 @@ PACK = 4
 TILES = V // P
 PASSAGES = U // D
 LIST_ROWS = 16
+QUADRANT = 32
+SCALE_ROWS = 4
 SLOPE = 6.0
 CUT = 0.4
 MEAN_WEIGHT = 0.25 / D
@@ -42,148 +44,146 @@ def tile_picked_yplaid_mix_p_kernel(tc, x_words, x_scales, hT, offs, code, out):
         all_words = sb.tile([P, T], U32, name="all_words")
         all_scales = sb.tile([P, T], U8, name="all_scales")
         x_codes = sb.tile([P, S], U32, name="x_codes", align_bytes=64)
-        x_plane = sb.tile([P, S], U8, name="x_plane", align_bytes=64)
+        picked_scales = sb.tile([P, S], U8, name="picked_scales", align_bytes=64)
         ident = sb.tile([P, P], F32, name="ident")
         warm = sb.tile([P, 2], F32, name="warm")
-        u = [t[:] for t in tiles(sb, "u", [P, S], F32, align_bytes=64)]
+
+        scores = [t[:] for t in tiles(sb, "scores", [P, S], F32, align_bytes=64)]
         first_bf = sb.tile([P, PACK * P], BF16, name="first_bf", align_bytes=64)
-        late_bf = u[1].bitcast(BF16)
+        late_bf = scores[1].bitcast(BF16)
         early_raw = tiles(sb, "early_raw", [P, PACK, P], F32, count=2)
         late_raw = sb.tile([P, PACK, 2 * P], F32, name="late_raw")
         gate = [late_raw[:].rearrange("p j w -> p (j w)")[:, :S]]
         gate = gate + [t[:] for t in tiles(sb, "gate", [P, S], F32, count=TILES - 1)]
         h_raw = [early_raw[0][:], early_raw[1][:], late_raw[:, :, :P], late_raw[:, :, P:]]
-        h_bf = [first_bf[:], u[0][:, : PACK * P // 2].bitcast(BF16), late_bf[:, : PACK * P], late_bf[:, PACK * P :]]
+        h_bf = [
+            first_bf[:],
+            scores[0][:, : PACK * P // 2].bitcast(BF16),
+            late_bf[:, : PACK * P],
+            late_bf[:, PACK * P :],
+        ]
         h_codes = sb.tile([P, V], U32, name="h_codes", align_bytes=64)
-        h_plane = sb.tile([P, V], U8, name="h_plane", align_bytes=64)
+        h_scales = sb.tile([P, V], U8, name="h_scales", align_bytes=64)
         y = tiles(psum, "y", [P, S], F32)
         bias = tiles(sb, "bias", [P, 1], F32)
         p = [t[:] for t in tiles(sb, "p", [P, S], F32)]
-        gg = tiles(sb, "gg", [P, PASSAGES, D], F32)
-        tops = [t[:] for t in tiles(sb, "tops", [P, 1], F32, count=TILES - 1)] + [gg[0][:, PASSAGES - 1, D - 1 :]]
-        best_all = sb.tile([P, TILES, PASSAGES], F32, name="best_all")
-        res_all = sb.tile([P, TILES, PASSAGES], F32, name="res_all")
-        best = [best_all[:, i, :] for i in range(TILES)]
-        res = [res_all[:, i, :] for i in range(TILES)]
+        gathered = tiles(sb, "gathered", [P, PASSAGES, D], F32)
+        early_top = tiles(sb, "early_top", [P, 1], F32, count=2)
+        top = {0: early_top[0][:], 1: early_top[1][:], 3: gathered[0][:, PASSAGES - 1, D - 1 :]}
+        best = sb.tile([P, TILES, PASSAGES], F32, name="best")
+        res = sb.tile([P, TILES, PASSAGES], F32, name="res")
         out_view = out.rearrange("(i p) v -> p i v", p=P)
 
         nc.gpsimd.memset(all_scales[:].bitcast(I32), 0)
         nc.gpsimd.memset(warm[:, 0:1], 0.0)
+
         h_view = hT.rearrange("(p j) w -> p j w", j=PACK)
         nc.sync.dma_start(offs_sb[:], offs)
-        for q in range(4):
-            (nc.sync if q < 2 else nc.scalar).dma_start(
-                all_scales[32 * q : 32 * q + 4, :].bitcast(I32),
-                x_scales[0, 4 * q : 4 * q + 4, :].bitcast(I32),
+        for q in range(P // QUADRANT):
+            queue = nc.sync if q < 2 else nc.scalar
+            queue.dma_start(
+                all_scales[QUADRANT * q : QUADRANT * q + SCALE_ROWS, :].bitcast(I32),
+                x_scales[0, SCALE_ROWS * q : SCALE_ROWS * (q + 1), :].bitcast(I32),
             )
         nc.sync.dma_start(all_words[:].bitcast(I32), x_words[0].rearrange("p n t -> p (n t)").bitcast(I32))
-        nc.sync.dma_start(h_raw[0], h_view[:, :, 0 * P : 1 * P])
-        nc.sync.dma_start(h_raw[1], h_view[:, :, 1 * P : 2 * P])
+        for i in range(2):
+            nc.sync.dma_start(h_raw[i], h_view[:, :, i * P : (i + 1) * P])
         nc.sync.dma_start(late_raw[:], h_view[:, :, 2 * P :])
         nc.sync.dma_start(code_sb[:], code)
         nc.scalar.activation(warm[:, 1:2], warm[:, 0:1], ACT.Sigmoid)
         make_identity(nc, ident[:])
 
-        def round_on_scalar(i):
-            nc.scalar.copy(h_bf[i].rearrange("p (w j) -> p w j", j=PACK), h_raw[i].rearrange("p j w -> p w j"))
-
-        def round_on_gpsimd(i):
-            nc.gpsimd.tensor_scalar(h_bf[i].rearrange("p (w j) -> p w j", j=PACK), h_raw[i].rearrange("p j w -> p w j"), 1.0, 0.0, ALU.mult, ALU.add)
+        def side_by_side(i):
+            return h_bf[i].rearrange("p (w j) -> p w j", j=PACK), h_raw[i].rearrange("p j w -> p w j")
 
         def quantise(tokens, src):
-            nc.vector.quantize_mx(out=h_codes[:, tokens].bitcast(FP8X4), scales=h_plane[:, tokens], in_=src)
+            nc.vector.quantize_mx(out=h_codes[:, tokens].bitcast(FP8X4), scales=h_scales[:, tokens], in_=src)
 
         def score(i):
             nc.tensor.matmul_mx(
                 out=y[i][:],
                 lhsT=h_codes[:, i * P : (i + 1) * P].bitcast(FP8X4),
-                lhsT_scale=h_plane[:, i * P : (i + 1) * P],
+                lhsT_scale=h_scales[:, i * P : (i + 1) * P],
                 rhs=x_codes[:].bitcast(FP8X4),
-                rhs_scale=x_plane[:],
+                rhs_scale=picked_scales[:],
                 start=True,
                 stop=True,
             )
 
         def gate_keeping_y(i, parts=(slice(0, S),)):
-            nc.vector.tensor_scalar(u[i], y[i][:], 1.0, None, ALU.mult, ALU.max, accum_out=tops[i])
-            nc.scalar.activation(bias[i][:], tops[i], ACT.Copy, scale=-SLOPE * CUT)
+            nc.vector.tensor_scalar(scores[i], y[i][:], 1.0, None, ALU.mult, ALU.max, accum_out=top[i])
+            nc.scalar.activation(bias[i][:], top[i], ACT.Copy, scale=-SLOPE * CUT)
             for cols in parts:
-                nc.scalar.activation(gate[i][:, cols], u[i][:, cols], ACT.Sigmoid, bias=bias[i][:], scale=SLOPE)
+                nc.scalar.activation(gate[i][:, cols], scores[i][:, cols], ACT.Sigmoid, bias=bias[i][:], scale=SLOPE)
 
         def gate_from_scaled_y(i):
-            nc.vector.tensor_scalar(u[i], y[i][:], -SLOPE * CUT, None, ALU.mult, ALU.min, accum_out=bias[i][:])
-            nc.scalar.activation(gate[i], u[i], ACT.Sigmoid, bias=bias[i][:], scale=-1.0 / CUT)
+            nc.vector.tensor_scalar(scores[i], y[i][:], -SLOPE * CUT, None, ALU.mult, ALU.min, accum_out=bias[i][:])
+            nc.scalar.activation(gate[i], scores[i], ACT.Sigmoid, bias=bias[i][:], scale=-1.0 / CUT)
 
         def fade_on_gpsimd(i, cols=slice(0, S)):
-            nc.gpsimd.tensor_tensor(p[i][:, cols], u[i][:, cols], gate[i][:, cols], ALU.mult)
-
-        def fade_on_vector(i, cols=slice(0, S)):
-            nc.vector.tensor_tensor(p[i][:, cols], y[i][:, cols], gate[i][:, cols], ALU.mult)
+            nc.gpsimd.tensor_tensor(p[i][:, cols], scores[i][:, cols], gate[i][:, cols], ALU.mult)
 
         halves = [slice(h * PASSAGES // 2, (h + 1) * PASSAGES // 2) for h in range(2)]
 
-        def window(i, h):
+        def look_up(i, h):
             half = halves[h]
             entries = code_sb[:, half.start * D // LIST_ROWS : half.stop * D // LIST_ROWS]
-            return gg[i][:, half, :].rearrange("p v d -> p (v d)"), p[i].indirect(entries)
+            return gathered[i][:, half, :].rearrange("p v d -> p (v d)"), p[i].indirect(entries)
 
         def fetch_on_vector(i, h):
-            nc.vector.tensor_copy(*window(i, h))
+            nc.vector.tensor_copy(*look_up(i, h))
 
         def fetch_on_scalar(i, h):
-            nc.scalar.activation(*window(i, h), ACT.Copy)
+            nc.scalar.activation(*look_up(i, h), ACT.Copy)
 
-        def largest(i, h):
-            nc.vector.tensor_reduce(best[i][:, halves[h]], gg[i][:, halves[h], :], AXIS_X, ALU.max)
+        def largest(i, passages=slice(0, PASSAGES)):
+            nc.vector.tensor_reduce(best[:, i, passages], gathered[i][:, passages, :], AXIS_X, ALU.max)
 
-        def means_on_tensor(first, count):
-            sum_t = psum.tile([P, count, P], F32, name=f"sum_t{first}")
-            for n in range(count):
-                for d in range(D):
-                    nc.tensor.matmul(
-                        sum_t[:, n, :], gg[first + n][:, :, d], ident[:], start=(d == 0), stop=(d == D - 1), is_transpose=True
-                    )
-            mean_t = sb.tile([P, count, P], F32, name=f"mean_t{first}")
+        def mean_on_tensor(i):
+            sum_t = psum.tile([P, P], F32, name=f"sum_t{i}")
+            for d in range(D):
+                nc.tensor.matmul(
+                    sum_t[:], gathered[i][:, :, d], ident[:], start=(d == 0), stop=(d == D - 1), is_transpose=True
+                )
+            mean_t = sb.tile([P, P], F32, name=f"mean_t{i}")
             nc.scalar.activation(mean_t[:], sum_t[:], ACT.Copy, scale=MEAN_WEIGHT)
-            back = psum.tile([P, count, P], F32, name=f"back{first}")
-            for n in range(count):
-                nc.tensor.transpose(back[:, n, :], mean_t[:, n, :], ident[:])
-            return back
+            mean = psum.tile([P, P], F32, name=f"mean{i}")
+            nc.tensor.transpose(mean[:], mean_t[:], ident[:])
+            return mean
 
-        def finish(first, count, back):
-            rows = slice(first, first + count)
-            nc.vector.tensor_tensor(res_all[:, rows, :], back[:], best_all[:, rows, :], ALU.add)
-            nc.sync.dma_start(out_view[:, rows, :], res_all[:, rows, :])
+        def finish_from_mean(i, mean):
+            nc.vector.tensor_tensor(res[:, i, :], mean[:], best[:, i, :], ALU.add)
+            nc.sync.dma_start(out_view[:, i, :], res[:, i, :])
 
-        pair_sum = sb.tile([P, PASSAGES, 2], F32, name="pair_sum")
-        late_sum = sb.tile([P, 2, PASSAGES], F32, name="late_sum")
-
-        def largest_whole(i):
-            nc.vector.tensor_reduce(best[i], gg[i][:], AXIS_X, ALU.max)
+        pair_sum = sb.tile([P, 2, PASSAGES, 2], F32, name="pair_sum")
+        sums = sb.tile([P, 2, PASSAGES], F32, name="sums")
 
         def sums_on_gpsimd(i, h):
-            half = halves[h]
-            nc.gpsimd.tensor_tensor(pair_sum[:, half, :], gg[i][:, half, 0:2], gg[i][:, half, 2:4], ALU.add)
-            nc.gpsimd.tensor_tensor(late_sum[:, i // 2, half], pair_sum[:, half, 0], pair_sum[:, half, 1], ALU.add)
-
-        def finish_from_sums(i):
-            nc.vector.scalar_tensor_tensor(res[i], late_sum[:, i // 2, :], MEAN_WEIGHT, best[i], ALU.mult, ALU.add)
-            nc.sync.dma_start(out[i * P : (i + 1) * P, :], res[i])
+            pairs = pair_sum[:, i // 2, halves[h], :]
+            values = gathered[i][:, halves[h], :]
+            nc.gpsimd.tensor_tensor(pairs, values[:, :, 0:2], values[:, :, 2:4], ALU.add)
+            nc.gpsimd.tensor_tensor(sums[:, i // 2, halves[h]], pairs[:, :, 0], pairs[:, :, 1], ALU.add)
 
         def sums_on_vector(i, h):
-            nc.vector.tensor_reduce(late_sum[:, i // 2, halves[h]], gg[i][:, halves[h], :], AXIS_X, ALU.add)
+            nc.vector.tensor_reduce(sums[:, i // 2, halves[h]], gathered[i][:, halves[h], :], AXIS_X, ALU.add)
+
+        def finish_from_sums(i):
+            nc.vector.scalar_tensor_tensor(
+                res[:, i, :], sums[:, i // 2, :], MEAN_WEIGHT, best[:, i, :], ALU.mult, ALU.add
+            )
+            nc.sync.dma_start(out[i * P : (i + 1) * P, :], res[:, i, :])
+
+        for i in range(TILES - 1):
+            nc.scalar.copy(*side_by_side(i))
+        nc.gpsimd.tensor_scalar(*side_by_side(TILES - 1), 1.0, 0.0, ALU.mult, ALU.add)
+
+        nc.vector.tensor_copy(picked_scales[:], all_scales[:].indirect(offs_sb[:]))
+        nc.vector.tensor_copy(x_codes[:], all_words[:].indirect(offs_sb[:]))
 
         column_halves = (slice(0, S // 2), slice(S // 2, S))
-        round_on_scalar(0)
-        round_on_scalar(1)
-        round_on_scalar(2)
-        round_on_gpsimd(3)
-        nc.vector.tensor_copy(x_plane[:], all_scales[:].indirect(offs_sb[:]))
-        nc.vector.tensor_copy(x_codes[:], all_words[:].indirect(offs_sb[:]))
-        quantise(slice(0, P), h_bf[0])
-        score(0)
-        quantise(slice(P, 2 * P), h_bf[1])
-        score(1)
+        for i in range(2):
+            quantise(slice(i * P, (i + 1) * P), h_bf[i])
+            score(i)
         gate_keeping_y(0, column_halves)
         quantise(slice(2 * P, V), late_bf)
         score(2)
@@ -195,28 +195,30 @@ def tile_picked_yplaid_mix_p_kernel(tc, x_words, x_scales, hT, offs, code, out):
         gate_from_scaled_y(2)
         gate_keeping_y(3)
         fade_on_gpsimd(3)
+
         fetch_on_vector(0, 0)
         fetch_on_scalar(0, 1)
-        fade_on_vector(2)
-        largest(0, 0)
+        nc.vector.tensor_tensor(p[2], y[2][:], gate[2], ALU.mult)
+        largest(0, halves[0])
         fetch_on_vector(2, 0)
         fetch_on_scalar(1, 1)
-        largest(0, 1)
+        largest(0, halves[1])
         fetch_on_scalar(2, 1)
-        back0 = means_on_tensor(0, 1)
+        mean0 = mean_on_tensor(0)
         fetch_on_vector(1, 0)
         sums_on_gpsimd(1, 1)
         sums_on_gpsimd(1, 0)
         fetch_on_scalar(3, 0)
-        back2 = means_on_tensor(2, 1)
+        sums_on_gpsimd(3, 0)
+        mean2 = mean_on_tensor(2)
         fetch_on_scalar(3, 1)
-        largest_whole(2)
-        largest_whole(1)
-        finish(0, 1, back0)
-        largest(3, 0)
-        sums_on_vector(3, 0)
-        largest(3, 1)
+
+        largest(2)
+        largest(1)
+        finish_from_mean(0, mean0)
+        largest(3, halves[0])
+        largest(3, halves[1])
         sums_on_vector(3, 1)
         finish_from_sums(1)
-        finish(2, 1, back2)
+        finish_from_mean(2, mean2)
         finish_from_sums(3)

@@ -74,16 +74,17 @@ def tile_picked_yplaid_mix_p_kernel(tc, x_words, x_scales, hT, offs, code, out):
         res = sb.tile([P, TILES, PASSAGES], F32, name="res")
         out_view = out.rearrange("(i p) v -> p i v", p=P)
 
-        nc.gpsimd.memset(all_scales[:].bitcast(I32), 0)
         nc.gpsimd.memset(warm[:, 0:1], 0.0)
 
         h_view = hT.rearrange("(p j) w -> p j w", j=PACK)
         nc.sync.dma_start(offs_sb[:], offs)
+        quadrant_rows = x_scales[0].rearrange("(q r) n -> q (r n)", r=SCALE_ROWS).bitcast(I32)
+        repeats = QUADRANT // SCALE_ROWS
         for q in range(P // QUADRANT):
             queue = nc.sync if q < 2 else nc.scalar
             queue.dma_start(
-                all_scales[QUADRANT * q : QUADRANT * q + SCALE_ROWS, :].bitcast(I32),
-                x_scales[0, SCALE_ROWS * q : SCALE_ROWS * (q + 1), :].bitcast(I32),
+                all_scales[QUADRANT * q : QUADRANT * (q + 1), :].bitcast(I32),
+                quadrant_rows[q : q + 1, :].to_broadcast([repeats, SCALE_ROWS * T // 4]),
             )
         nc.sync.dma_start(all_words[:].bitcast(I32), x_words[0].rearrange("p n t -> p (n t)").bitcast(I32))
         for i in range(2):

@@ -97,6 +97,12 @@ def tile_picked_yplaid_mix_p_kernel(tc, x_words, x_scales, hT, offs, code, out):
         def side_by_side(i):
             return h_bf[i].rearrange("p (w j) -> p w j", j=PACK), h_raw[i].rearrange("p j w -> p w j")
 
+        def side_by_side_in_lines(i):
+            return (
+                h_bf[i].rearrange("p (c n j) -> p c j n", n=PACK, j=PACK),
+                h_raw[i].rearrange("p j (c n) -> p c j n", n=PACK),
+            )
+
         def quantise(tokens, src):
             nc.vector.quantize_mx(out=h_codes[:, tokens].bitcast(FP8X4), scales=h_scales[:, tokens], in_=src)
 
@@ -175,7 +181,7 @@ def tile_picked_yplaid_mix_p_kernel(tc, x_words, x_scales, hT, offs, code, out):
             nc.sync.dma_start(out[i * P : (i + 1) * P, :], res[:, i, :])
 
         for i in range(TILES - 1):
-            nc.scalar.copy(*side_by_side(i))
+            nc.scalar.copy(*side_by_side_in_lines(i))
         nc.gpsimd.tensor_scalar(*side_by_side(TILES - 1), 1.0, 0.0, ALU.mult, ALU.add)
 
         nc.vector.tensor_copy(picked_scales[:], all_scales[:].indirect(offs_sb[:]))

@@ -165,11 +165,11 @@ def tile_picked_yplaid_mix_p_kernel(tc, x_words, x_scales, hT, offs, code, out):
         pair_sum = sb.tile([P, 2, PASSAGES, 2], F32, name="pair_sum")
         sums = sb.tile([P, 2, PASSAGES], F32, name="sums")
 
-        def sums_on_gpsimd(i, h):
-            pairs = pair_sum[:, i // 2, halves[h], :]
-            values = gathered[i][:, halves[h], :]
+        def sums_on_gpsimd(i, part):
+            pairs = pair_sum[:, i // 2, part, :]
+            values = gathered[i][:, part, :]
             nc.gpsimd.tensor_tensor(pairs, values[:, :, 0:2], values[:, :, 2:4], ALU.add)
-            nc.gpsimd.tensor_tensor(sums[:, i // 2, halves[h]], pairs[:, :, 0], pairs[:, :, 1], ALU.add)
+            nc.gpsimd.tensor_tensor(sums[:, i // 2, part], pairs[:, :, 0], pairs[:, :, 1], ALU.add)
 
         def sums_on_vector(i, h):
             nc.vector.tensor_reduce(sums[:, i // 2, halves[h]], gathered[i][:, halves[h], :], AXIS_X, ALU.add)
@@ -187,7 +187,7 @@ def tile_picked_yplaid_mix_p_kernel(tc, x_words, x_scales, hT, offs, code, out):
         nc.vector.tensor_copy(picked_scales[:], all_scales[:].indirect(offs_sb[:]))
         nc.vector.tensor_copy(x_codes[:], all_words[:].indirect(offs_sb[:]))
 
-        column_halves = (slice(0, S // 2), slice(S // 2, S))
+        column_halves = (slice(0, S // 4), slice(S // 4, S))
         for i in range(2):
             quantise(slice(i * P, (i + 1) * P), h_bf[i])
             score(i)
@@ -213,10 +213,9 @@ def tile_picked_yplaid_mix_p_kernel(tc, x_words, x_scales, hT, offs, code, out):
         fetch_on_scalar(2, 1)
         mean0 = mean_on_tensor(0)
         fetch_on_vector(1, 0)
-        sums_on_gpsimd(1, 1)
-        sums_on_gpsimd(1, 0)
+        sums_on_gpsimd(1, slice(0, PASSAGES))
         fetch_on_scalar(3, 0)
-        sums_on_gpsimd(3, 0)
+        sums_on_gpsimd(3, halves[0])
         mean2 = mean_on_tensor(2)
         fetch_on_scalar(3, 1)
 

@@ -165,11 +165,14 @@ def tile_picked_yplaid_mix_p_kernel(tc, x_words, x_scales, hT, offs, code, out):
         pair_sum = sb.tile([P, 2, PASSAGES, 2], F32, name="pair_sum")
         sums = sb.tile([P, 2, PASSAGES], F32, name="sums")
 
-        def sums_on_gpsimd(i, part):
-            pairs = pair_sum[:, i // 2, part, :]
+        def pairs_on_gpsimd(i, part):
             values = gathered[i][:, part, :]
-            nc.gpsimd.tensor_tensor(pairs, values[:, :, 0:2], values[:, :, 2:4], ALU.add)
-            nc.gpsimd.tensor_tensor(sums[:, i // 2, part], pairs[:, :, 0], pairs[:, :, 1], ALU.add)
+            nc.gpsimd.tensor_tensor(pair_sum[:, i // 2, part, :], values[:, :, 0:2], values[:, :, 2:4], ALU.add)
+
+        def join_pairs_on_gpsimd(count):
+            pairs = pair_sum[:].rearrange("p i v e -> p (i v) e")[:, :count, :]
+            flat = sums[:].rearrange("p i v -> p (i v)")[:, :count]
+            nc.gpsimd.tensor_tensor(flat, pairs[:, :, 0], pairs[:, :, 1], ALU.add)
 
         def sums_on_vector(i, h):
             nc.vector.tensor_reduce(sums[:, i // 2, halves[h]], gathered[i][:, halves[h], :], AXIS_X, ALU.add)
@@ -213,9 +216,10 @@ def tile_picked_yplaid_mix_p_kernel(tc, x_words, x_scales, hT, offs, code, out):
         fetch_on_scalar(2, 1)
         mean0 = mean_on_tensor(0)
         fetch_on_vector(1, 0)
-        sums_on_gpsimd(1, slice(0, PASSAGES))
+        pairs_on_gpsimd(1, slice(0, PASSAGES))
         fetch_on_scalar(3, 0)
-        sums_on_gpsimd(3, halves[0])
+        pairs_on_gpsimd(3, halves[0])
+        join_pairs_on_gpsimd(PASSAGES + PASSAGES // 2)
         mean2 = mean_on_tensor(2)
         fetch_on_scalar(3, 1)
 

@@ -26,6 +26,7 @@ QUADRANT = 32
 SCALE_ROWS = 4
 SLOPE = 6.0
 CUT = 0.4
+LATE_ON_SCALAR = 160
 MEAN_WEIGHT = 0.25 / D
 
 
@@ -55,13 +56,8 @@ def tile_picked_yplaid_mix_p_kernel(tc, x_words, x_scales, hT, offs, code, out):
         late_raw = sb.tile([P, PACK, 2 * P], F32, name="late_raw")
         gate = [late_raw[:].rearrange("p j w -> p (j w)")[:, :S]]
         gate = gate + [t[:] for t in tiles(sb, "gate", [P, S], F32, count=TILES - 1)]
-        h_raw = [early_raw[0][:], early_raw[1][:], late_raw[:, :, :P], late_raw[:, :, P:]]
-        h_bf = [
-            first_bf[:],
-            scores[0][:, : PACK * P // 2].bitcast(BF16),
-            late_bf[:, : PACK * P],
-            late_bf[:, PACK * P :],
-        ]
+        h_raw = [early_raw[0][:], early_raw[1][:]]
+        h_bf = [first_bf[:], scores[0][:, : PACK * P // 2].bitcast(BF16)]
         h_codes = sb.tile([P, V], U32, name="h_codes", align_bytes=64)
         h_scales = sb.tile([P, V], U8, name="h_scales", align_bytes=64)
         y = tiles(psum, "y", [P, S], F32)
@@ -94,13 +90,13 @@ def tile_picked_yplaid_mix_p_kernel(tc, x_words, x_scales, hT, offs, code, out):
         nc.scalar.activation(warm[:, 1:2], warm[:, 0:1], ACT.Sigmoid)
         make_identity(nc, ident[:])
 
-        def side_by_side(i):
-            return h_bf[i].rearrange("p (w j) -> p w j", j=PACK), h_raw[i].rearrange("p j w -> p w j")
+        def side_by_side(rounded, raw):
+            return rounded.rearrange("p (w j) -> p w j", j=PACK), raw.rearrange("p j w -> p w j")
 
-        def side_by_side_in_lines(i):
+        def side_by_side_in_lines(rounded, raw):
             return (
-                h_bf[i].rearrange("p (c n j) -> p c j n", n=PACK, j=PACK),
-                h_raw[i].rearrange("p j (c n) -> p c j n", n=PACK),
+                rounded.rearrange("p (c n j) -> p c j n", n=PACK, j=PACK),
+                raw.rearrange("p j (c n) -> p c j n", n=PACK),
             )
 
         def quantise(tokens, src):
@@ -183,9 +179,13 @@ def tile_picked_yplaid_mix_p_kernel(tc, x_words, x_scales, hT, offs, code, out):
             )
             nc.sync.dma_start(out[i * P : (i + 1) * P, :], res[:, i, :])
 
-        for i in range(TILES - 1):
-            nc.scalar.copy(*side_by_side_in_lines(i))
-        nc.gpsimd.tensor_scalar(*side_by_side(TILES - 1), 1.0, 0.0, ALU.mult, ALU.add)
+        for i in range(2):
+            nc.scalar.copy(*side_by_side_in_lines(h_bf[i], h_raw[i]))
+        cut = PACK * LATE_ON_SCALAR
+        nc.scalar.copy(*side_by_side_in_lines(late_bf[:, :cut], late_raw[:, :, :LATE_ON_SCALAR]))
+        nc.gpsimd.tensor_scalar(
+            *side_by_side(late_bf[:, cut:], late_raw[:, :, LATE_ON_SCALAR:]), 1.0, 0.0, ALU.mult, ALU.add
+        )
 
         nc.vector.tensor_copy(picked_scales[:], all_scales[:].indirect(offs_sb[:]))
         nc.vector.tensor_copy(x_codes[:], all_words[:].indirect(offs_sb[:]))

from contextlib import ExitStack

import concourse.mybir as mybir
from concourse.masks import make_identity

K, T, S, V, U, D = 512, 1024, 512, 512, 512, 4
FLOPS = 2 * K * V * S

F32 = mybir.dt.float32
BF16 = mybir.dt.bfloat16
I32 = mybir.dt.int32
U32 = mybir.dt.uint32
U16 = mybir.dt.uint16
U8 = mybir.dt.uint8
FP8X4 = mybir.dt.float8_e4m3fn_x4
ALU = mybir.AluOpType
ACT = mybir.ActivationFunctionType
AXIS_X = mybir.AxisListType.X

P = 128
PACK = 4
TILES = V // P
PASSAGES = U // D
LIST_ROWS = 16
QUADRANT = 32
SCALE_ROWS = 4
SLOPE = 6.0
CUT = 0.4
LATE_ON_SCALAR = 160
MEAN_WEIGHT = 0.25 / D


def tile_picked_yplaid_mix_p_kernel(tc, x_words, x_scales, hT, offs, code, out):
    nc = tc.nc
    with ExitStack() as ctx:
        lists = ctx.enter_context(tc.tile_pool(name="lists", bufs=1))
        sb = ctx.enter_context(tc.tile_pool(name="sb", bufs=1))
        psum = ctx.enter_context(tc.psum_pool(name="psum", bufs=1))

        def tiles(pool, stem, shape, dtype, count=TILES, **kw):
            return [pool.tile(shape, dtype, name=f"{stem}{i}", **kw) for i in range(count)]

        offs_sb = lists.tile([P, S // LIST_ROWS], U16, name="offs_sb")
        code_sb = lists.tile([P, U // LIST_ROWS], U16, name="code_sb")
        all_words = sb.tile([P, T], U32, name="all_words")
        all_scales = sb.tile([P, T], U8, name="all_scales")
        x_codes = sb.tile([P, S], U32, name="x_codes", align_bytes=64)
        picked_scales = sb.tile([P, S], U8, name="picked_scales", align_bytes=64)
        ident = sb.tile([P, P], F32, name="ident")
        warm = sb.tile([P, 2], F32, name="warm")

        scores = [t[:] for t in tiles(sb, "scores", [P, S], F32, align_bytes=64)]
        first_bf = sb.tile([P, PACK * P], BF16, name="first_bf", align_bytes=64)
        late_bf = scores[1].bitcast(BF16)
        early_raw = tiles(sb, "early_raw", [P, PACK, P], F32, count=2)
        late_raw = sb.tile([P, PACK, 2 * P], F32, name="late_raw")
        gate = [late_raw[:].rearrange("p j w -> p (j w)")[:, :S]]
        gate = gate + [t[:] for t in tiles(sb, "gate", [P, S], F32, count=TILES - 1)]
        h_raw = [early_raw[0][:], early_raw[1][:]]
        h_bf = [first_bf[:], scores[0][:, : PACK * P // 2].bitcast(BF16)]
        h_codes = sb.tile([P, V], U32, name="h_codes", align_bytes=64)
        h_scales = sb.tile([P, V], U8, name="h_scales", align_bytes=64)
        y = tiles(psum, "y", [P, S], F32)
        bias = tiles(sb, "bias", [P, 1], F32)
        p = [t[:] for t in tiles(sb, "p", [P, S], F32)]
        gathered = tiles(sb, "gathered", [P, PASSAGES, D], F32)
        early_top = tiles(sb, "early_top", [P, 1], F32, count=2)
        top = {0: early_top[0][:], 1: early_top[1][:], 3: gathered[0][:, PASSAGES - 1, D - 1 :]}
        best = sb.tile([P, TILES, PASSAGES], F32, name="best")
        res = sb.tile([P, TILES, PASSAGES], F32, name="res")
        out_view = out.rearrange("(i p) v -> p i v", p=P)

        nc.gpsimd.memset(warm[:, 0:1], 0.0)

        h_view = hT.rearrange("(p j) w -> p j w", j=PACK)
        nc.sync.dma_start(offs_sb[:], offs)
        quadrant_rows = x_scales[0].rearrange("(q r) n -> q (r n)", r=SCALE_ROWS).bitcast(I32)
        repeats = QUADRANT // SCALE_ROWS
        for q in range(P // QUADRANT):
            queue = nc.sync if q < 2 else nc.scalar
            queue.dma_start(
                all_scales[QUADRANT * q : QUADRANT * (q + 1), :].bitcast(I32),
                quadrant_rows[q : q + 1, :].to_broadcast([repeats, SCALE_ROWS * T // 4]),
            )
        nc.sync.dma_start(all_words[:].bitcast(I32), x_words[0].rearrange("p n t -> p (n t)").bitcast(I32))
        for i in range(2):
            nc.sync.dma_start(h_raw[i], h_view[:, :, i * P : (i + 1) * P])
        nc.sync.dma_start(late_raw[:], h_view[:, :, 2 * P :])
        nc.sync.dma_start(code_sb[:], code)
        nc.scalar.activation(warm[:, 1:2], warm[:, 0:1], ACT.Sigmoid)
        make_identity(nc, ident[:])

        def side_by_side(rounded, raw):
            return rounded.rearrange("p (w j) -> p w j", j=PACK), raw.rearrange("p j w -> p w j")

        def side_by_side_in_lines(rounded, raw):
            return (
                rounded.rearrange("p (c n j) -> p c j n", n=PACK, j=PACK),
                raw.rearrange("p j (c n) -> p c j n", n=PACK),
            )

        def quantise(tokens, src):
            nc.vector.quantize_mx(out=h_codes[:, tokens].bitcast(FP8X4), scales=h_scales[:, tokens], in_=src)

        def score(i):
            nc.tensor.matmul_mx(
                out=y[i][:],
                lhsT=h_codes[:, i * P : (i + 1) * P].bitcast(FP8X4),
                lhsT_scale=h_scales[:, i * P : (i + 1) * P],
                rhs=x_codes[:].bitcast(FP8X4),
                rhs_scale=picked_scales[:],
                start=True,
                stop=True,
            )

        def gate_keeping_y(i, parts=(slice(0, S),)):
            nc.vector.tensor_scalar(scores[i], y[i][:], 1.0, None, ALU.mult, ALU.max, accum_out=top[i])
            nc.scalar.activation(bias[i][:], top[i], ACT.Copy, scale=-SLOPE * CUT)
            for cols in parts:
                nc.scalar.activation(gate[i][:, cols], scores[i][:, cols], ACT.Sigmoid, bias=bias[i][:], scale=SLOPE)

        def gate_from_scaled_y(i):
            nc.vector.tensor_scalar(scores[i], y[i][:], -SLOPE * CUT, None, ALU.mult, ALU.min, accum_out=bias[i][:])
            nc.scalar.activation(gate[i], scores[i], ACT.Sigmoid, bias=bias[i][:], scale=-1.0 / CUT)

        def fade_on_gpsimd(i, cols=slice(0, S)):
            nc.gpsimd.tensor_tensor(p[i][:, cols], scores[i][:, cols], gate[i][:, cols], ALU.mult)

        halves = [slice(h * PASSAGES // 2, (h + 1) * PASSAGES // 2) for h in range(2)]

        def look_up(i, h):
            half = halves[h]
            entries = code_sb[:, half.start * D // LIST_ROWS : half.stop * D // LIST_ROWS]
            return gathered[i][:, half, :].rearrange("p v d -> p (v d)"), p[i].indirect(entries)

        def fetch_on_vector(i, h):
            nc.vector.tensor_copy(*look_up(i, h))

        def fetch_on_scalar(i, h):
            nc.scalar.activation(*look_up(i, h), ACT.Copy)

        def largest(i, passages=slice(0, PASSAGES)):
            nc.vector.tensor_reduce(best[:, i, passages], gathered[i][:, passages, :], AXIS_X, ALU.max)

        def mean_on_tensor(i):
            sum_t = psum.tile([P, P], F32, name=f"sum_t{i}")
            for d in range(D):
                nc.tensor.matmul(
                    sum_t[:], gathered[i][:, :, d], ident[:], start=(d == 0), stop=(d == D - 1), is_transpose=True
                )
            mean_t = sb.tile([P, P], F32, name=f"mean_t{i}")
            nc.scalar.activation(mean_t[:], sum_t[:], ACT.Copy, scale=MEAN_WEIGHT)
            mean = psum.tile([P, P], F32, name=f"mean{i}")
            nc.tensor.transpose(mean[:], mean_t[:], ident[:])
            return mean

        def finish_from_mean(i, mean):
            nc.vector.tensor_tensor(res[:, i, :], mean[:], best[:, i, :], ALU.add)
            nc.sync.dma_start(out_view[:, i, :], res[:, i, :])

        pair_sum = sb.tile([P, 2, PASSAGES, 2], F32, name="pair_sum")
        sums = sb.tile([P, 2, PASSAGES], F32, name="sums")

        def pairs_on_gpsimd(i, part):
            values = gathered[i][:, part, :]
            nc.gpsimd.tensor_tensor(pair_sum[:, i // 2, part, :], values[:, :, 0:2], values[:, :, 2:4], ALU.add)

        def join_pairs_on_gpsimd(count):
            pairs = pair_sum[:].rearrange("p i v e -> p (i v) e")[:, :count, :]
            flat = sums[:].rearrange("p i v -> p (i v)")[:, :count]
            nc.gpsimd.tensor_tensor(flat, pairs[:, :, 0], pairs[:, :, 1], ALU.add)

        def sums_on_vector(i, h):
            nc.vector.tensor_reduce(sums[:, i // 2, halves[h]], gathered[i][:, halves[h], :], AXIS_X, ALU.add)

        def finish_from_sums(i):
            nc.vector.scalar_tensor_tensor(
                res[:, i, :], sums[:, i // 2, :], MEAN_WEIGHT, best[:, i, :], ALU.mult, ALU.add
            )
            nc.sync.dma_start(out[i * P : (i + 1) * P, :], res[:, i, :])

        for i in range(2):
            nc.scalar.copy(*side_by_side_in_lines(h_bf[i], h_raw[i]))
        cut = PACK * LATE_ON_SCALAR
        nc.scalar.copy(*side_by_side_in_lines(late_bf[:, :cut], late_raw[:, :, :LATE_ON_SCALAR]))
        nc.gpsimd.tensor_scalar(
            *side_by_side(late_bf[:, cut:], late_raw[:, :, LATE_ON_SCALAR:]), 1.0, 0.0, ALU.mult, ALU.add
        )

        nc.vector.tensor_copy(picked_scales[:], all_scales[:].indirect(offs_sb[:]))
        nc.vector.tensor_copy(x_codes[:], all_words[:].indirect(offs_sb[:]))

        column_halves = (slice(0, S // 4), slice(S // 4, S))
        for i in range(2):
            quantise(slice(i * P, (i + 1) * P), h_bf[i])
            score(i)
        gate_keeping_y(0, column_halves)
        quantise(slice(2 * P, V), late_bf)
        score(2)
        score(3)
        for cols in column_halves:
            fade_on_gpsimd(0, cols)
        gate_keeping_y(1)
        fade_on_gpsimd(1)
        gate_from_scaled_y(2)
        gate_keeping_y(3)
        fade_on_gpsimd(3)

        fetch_on_vector(0, 0)
        fetch_on_scalar(0, 1)
        nc.vector.tensor_tensor(p[2], y[2][:], gate[2], ALU.mult)
        largest(0, halves[0])
        fetch_on_vector(2, 0)
        fetch_on_scalar(1, 1)
        largest(0, halves[1])
        fetch_on_scalar(2, 1)
        mean0 = mean_on_tensor(0)
        fetch_on_vector(1, 0)
        pairs_on_gpsimd(1, slice(0, PASSAGES))
        fetch_on_scalar(3, 0)
        pairs_on_gpsimd(3, halves[0])
        join_pairs_on_gpsimd(PASSAGES + PASSAGES // 2)
        mean2 = mean_on_tensor(2)
        fetch_on_scalar(3, 1)

        largest(2)
        largest(1)
        finish_from_mean(0, mean0)
        largest(3, halves[0])
        largest(3, halves[1])
        sums_on_vector(3, 1)
        finish_from_sums(1)
        finish_from_mean(2, mean2)
        finish_from_sums(3)
